import numpy as np
import ml_dtypes


def mxq(x, axis, fmt="e4m3"):
    dtype, down = {"e4m3": (ml_dtypes.float8_e4m3fn, 7), "e5m2": (ml_dtypes.float8_e5m2, 14)}[fmt]
    v = np.moveaxis(np.asarray(x, np.float32).astype(ml_dtypes.bfloat16).astype(np.float64), axis, -1)
    blocks = v.reshape(v.shape[:-1] + (-1, 32))
    amax = np.abs(blocks).max(-1, keepdims=True)
    byte = np.maximum(np.where(amax > 0, np.frexp(amax)[1] - 1 + 127, 0) - down, 1)
    scale = np.exp2(byte - 127.0)
    codes = (blocks / scale).astype(np.float32).astype(dtype).astype(np.float64)
    return np.moveaxis((codes * scale).reshape(v.shape), -1, axis)


WIDE = False


def mx_kscale(k):
    if not WIDE:
        return np.ones(k)
    levels = np.array([10, -10, 5, -5, 0])
    if k % 512:
        return np.exp2(np.random.permutation(np.resize(levels, k // 32))).repeat(32)
    a = np.empty((k // 512, 16))
    for p in range(k // 512):
        a[p, :8] = np.random.permutation(np.resize(levels, 8))
        for g in range(8):
            far = levels[np.abs(levels - a[p, g]) >= 10]
            a[p, g + 8] = far[np.random.randint(len(far))]
    return np.exp2(a.ravel()).repeat(32)


BF16 = ml_dtypes.bfloat16


def bf(x):
    return np.asarray(x, np.float32).astype(BF16)


def f64(x):
    return np.asarray(x).astype(np.float64)

def planes(Y):
    n, m = Y.shape
    b = f64(bf(Y)).reshape(n // 32, 32, m)
    amax = np.abs(b).max(1)
    byte = np.clip(np.where(amax > 0, np.frexp(amax)[1] - 1 + 127 - 7, 1), 1, 254)
    codes = (b * np.exp2(127.0 - byte)[:, None, :]).reshape(n, m).astype(np.float32).astype(ml_dtypes.float8_e4m3fn).view(np.uint8)
    words = codes.reshape(n // 512, 128, 4, m).transpose(0, 1, 3, 2)
    return np.ascontiguousarray(words), np.ascontiguousarray(byte.astype(np.uint8).reshape(n // 512, 16, m))


N, D, C, O = 1024, 512, 2048, 1024


def centre_logits(x, a, m, p, lp):
    h = x * a
    k = (x * x - 1.0) * a
    hm = mxq(h, 1, "e4m3") @ mxq(m, 0, "e4m3")
    kp = mxq(k, 1, "e4m3") @ mxq(p, 0, "e4m3")
    return hm - kp + lp


def setup_inputs():
    s, t = mx_kscale(D), mx_kscale(C)
    return {
        "x": bf(np.random.standard_normal((N, D))),
        "a": bf((1.0 + 0.1 * np.random.standard_normal(D)) * s),
        "m": bf(np.random.standard_normal((D, C)) * (0.7 / np.sqrt(D)) / s[:, None]),
        "p": bf(np.random.standard_normal((D, C)) * (0.5 / np.sqrt(D)) / s[:, None]),
        "lp": bf(0.3 * np.random.standard_normal(C)),
        "gc": bf((1.0 + 0.1 * np.random.standard_normal(C)) * t),
        "w": bf(np.random.standard_normal((C, O)) / np.sqrt(C) / t[:, None]),
    }


def core(x, a, m, p, lp, gc, w):
    q = centre_logits(f64(x), f64(a), f64(m), f64(p), f64(lp))
    e = np.exp(q - q.max(-1, keepdims=True))
    phi = e / e.sum(-1, keepdims=True)
    num_centres = phi.shape[-1]
    r = (num_centres * phi - 1.0) * f64(gc)
    return mxq(r, 1, "e4m3") @ mxq(f64(w), 0, "e4m3")


def reference(x, a, m, p, lp, gc, w):
    R_out = core(x, a, m, p, lp, gc, w)
    words, scales = planes(R_out)
    return R_out, words, scales

@@ -1,0 +1,342 @@
+from contextlib import ExitStack
+
+import concourse.mybir as mybir
+from concourse.masks import make_identity
+
+N, D, C, O = 1024, 512, 2048, 1024
+FLOPS = 2 * N * D * C * 2 + 2 * N * C * O
+
+F32 = mybir.dt.float32
+BF16 = mybir.dt.bfloat16
+U32 = mybir.dt.uint32
+I32 = mybir.dt.int32
+U8 = mybir.dt.uint8
+FP8X4 = mybir.dt.float8_e4m3fn_x4
+ALU = mybir.AluOpType
+ACT = mybir.ActivationFunctionType
+AX = mybir.AxisListType
+
+P = 128
+BLOCKS = N // P
+CHUNK = 512
+CHUNKS = C // CHUNK
+GSTEP = 256
+NORM_S = ((6, 1), (7, 1))
+PASSES = C // 512
+
+
+def tile_ellipticalnormalizedrbfnet_x1_kernel(tc, x, a, m, p, lp, gc, w, out_0, out_1, out_2):
+    nc = tc.nc
+    with ExitStack() as ctx:
+        const = ctx.enter_context(tc.tile_pool(name="const", bufs=1))
+        keep = ctx.enter_context(tc.tile_pool(name="keep", bufs=1))
+        work = ctx.enter_context(tc.tile_pool(name="work", bufs=2))
+        psum = ctx.enter_context(tc.psum_pool(name="psum", bufs=2))
+
+        h_codes = keep.tile([P, N], U32, align_bytes=64)
+        h_scales = keep.tile([P, N], U8, align_bytes=64)
+        k_codes = keep.tile([P, N], U32, align_bytes=64)
+        k_scales = keep.tile([P, N], U8, align_bytes=64)
+        m_codes = keep.tile([P, C], U32, align_bytes=64)
+        m_scales = keep.tile([P, C], U8, align_bytes=64)
+        p_codes = keep.tile([P, C], U32, align_bytes=64)
+        p_scales = keep.tile([P, C], U8, align_bytes=64)
+        w_codes = keep.tile([P, PASSES, O], U32, align_bytes=64)
+        w_scales = keep.tile([P, PASSES, O], U8, align_bytes=64)
+        ident = const.tile([P, P], F32)
+        sel_lp = const.tile([P, P], BF16)
+        sel_gc = const.tile([P, P], BF16)
+        lp_all = const.tile([P, C], BF16)
+        gc_all = const.tile([P, C], BF16)
+        a_col = const.tile([P, 4], BF16)
+        a_neg = const.tile([P, 4], BF16)
+        warm = const.tile([P, 1], F32)
+        minus = const.tile([P, 1], F32)
+
+        x_view = x.rearrange("(g p t) d -> g p t d", g=2, t=4)
+        m_view = m.rearrange("(p j) c -> p j c", j=4)
+        p_view = p.rearrange("(p j) c -> p j c", j=4)
+        w_view = w.rearrange("(q p j) o -> q p j o", q=PASSES, j=4)
+
+        nc.vector.memset(warm[:], 0.0)
+        nc.vector.memset(minus[:], -1.0 / C)
+        nc.scalar.activation(out=warm[:], in_=warm[:], func=ACT.Exp)
+
+        x_sb = []
+        x0 = work.tile([P, 4, D], BF16, tag="x", bufs=2)
+        nc.sync.dma_start(out=x0[:], in_=x_view[0])
+        x_sb.append(x0)
+        nc.sync.dma_start(out=a_col[:], in_=a.rearrange("(p t) -> p t", t=4))
+        vec = work.tile([P, C], BF16, tag="x", bufs=2)
+        nc.vector.memset(vec[:], 0.0)
+        raw = {}
+
+        def load_mp(name, view, lo, hi):
+            r = work.tile([P, 4, 512], BF16, tag="raw4", bufs=6, name="raw4")
+            nc.sync.dma_start(out=r[:], in_=view[:, :, lo:hi])
+            for s in range(lo, hi, 512):
+                raw[(name, s // 512)] = r[:, :, s - lo : s - lo + 512]
+
+        load_mp("m", m_view, 0, 512)
+        load_mp("p", p_view, 0, 512)
+        nc.sync.dma_start(out=vec[0:1, :], in_=lp.unsqueeze(0))
+        nc.sync.dma_start(out=vec[32:33, :], in_=gc.unsqueeze(0))
+        for c in range(1, CHUNKS):
+            load_mp("m", m_view, 512 * c, 512 * c + 512)
+            load_mp("p", p_view, 512 * c, 512 * c + 512)
+
+        make_identity(nc, ident[:])
+        nc.gpsimd.memset(sel_lp[:], 0.0)
+        nc.gpsimd.memset(sel_lp[0:1, :], 1.0)
+        nc.gpsimd.memset(sel_gc[:], 0.0)
+        nc.gpsimd.memset(sel_gc[32:33, :], float(C))
+        nc.vector.tensor_scalar_mul(a_neg[:], a_col[:], -1.0)
+
+        def interleave(engine, dst, src):
+            n = dst.shape[1]
+            step = GSTEP if engine == "G" else n
+            for c0 in range(0, n, step):
+                d = dst[:, c0 : c0 + step].rearrange("p (c i) t -> p c t i", i=4)
+                s = src[:, :, c0 : c0 + step].rearrange("p t (c i) -> p c t i", i=4)
+                if engine == "V":
+                    nc.vector.tensor_copy(out=d, in_=s)
+                elif engine == "S":
+                    nc.scalar.copy(out=d, in_=s)
+                else:
+                    nc.gpsimd.tensor_scalar(out=d, in0=s, scalar1=1.0, scalar2=0.0, op0=ALU.mult, op1=ALU.add)
+
+        def bcast(sel, dst):
+            for h in range(2):
+                ps = psum.tile([P, 1024], BF16, tag="o", bufs=2, name="bc")
+                for s in range(2):
+                    c0 = h * 1024 + s * 512
+                    nc.tensor.matmul(ps[:, s * 512 : s * 512 + 512], lhsT=sel[:], rhs=vec[:, c0 : c0 + 512], start=True, stop=True)
+                nc.scalar.copy(out=dst[:, h * 1024 : h * 1024 + 1024], in_=ps[:])
+
+        a3 = a_col[:].rearrange("p (u e) -> p u e", e=2).unsqueeze(1).to_broadcast([P, 256, 2, 2])
+        n3 = a_neg[:].unsqueeze(1).to_broadcast([P, 256, 4])
+
+        def prep_pair(j):
+            g, t0 = divmod(2 * j, 4)
+            words = x_sb[g][:].bitcast(F32)
+            ps = psum.tile([P, 2, 256], F32, tag="tr", bufs=2, name="xt")
+            for b in range(2):
+                for u in range(2):
+                    nc.tensor.transpose(ps[:, u, b * P : b * P + P], words[:, t0 + b, u : 256 : 2], ident[:])
+            xt = ps[:].bitcast(BF16).rearrange("p u (r e) -> p r u e", e=2)
+            hb = work.tile([P, 256, 4], BF16, tag="hb", bufs=2, align_bytes=64, name="hb")
+            kb = work.tile([P, 256, 4], BF16, tag="kb", bufs=2, align_bytes=64, name="kb")
+            sq = work.tile([P, 256, 4], F32, tag="sq", bufs=1, name="sq")
+            nc.scalar.activation(out=sq[:].rearrange("p r (u e) -> p r u e", e=2), in_=xt, func=ACT.Square)
+            nc.vector.tensor_tensor(out=hb[:].rearrange("p r (u e) -> p r u e", e=2), in0=xt, in1=a3, op=ALU.mult)
+            nc.vector.scalar_tensor_tensor(out=kb[:], in0=sq[:], scalar=1.0, in1=n3, op0=ALU.subtract, op1=ALU.mult)
+            cols = slice(j * 256, j * 256 + 256)
+            nc.vector.quantize_mx(out=h_codes[:, cols].bitcast(FP8X4), scales=h_scales[:, cols], in_=hb[:].rearrange("p r t -> p (r t)"))
+            nc.vector.quantize_mx(out=k_codes[:, cols].bitcast(FP8X4), scales=k_scales[:, cols], in_=kb[:].rearrange("p r t -> p (r t)"))
+
+        il = {}
+
+        def mp_inter(name, c, engine):
+            t = work.tile([P, 512, 4], BF16, tag="il", bufs=3, align_bytes=64, name="il")
+            interleave(engine, t[:], raw[(name, c)])
+            il[(name, c)] = t
+
+        def mp_quant(name, c):
+            codes, scales = (m_codes, m_scales) if name == "m" else (p_codes, p_scales)
+            cols = slice(c * 512, c * 512 + 512)
+            nc.vector.quantize_mx(out=codes[:, cols].bitcast(FP8X4), scales=scales[:, cols], in_=il[(name, c)][:].rearrange("p c t -> p (c t)"))
+
+        w_raw = {}
+
+        def w_load(q):
+            r = work.tile([P, 4, 1024], BF16, tag="raw8", bufs=2, name="raw8")
+            nc.sync.dma_start(out=r[:], in_=w_view[q])
+            w_raw[q] = r
+
+        def w_inter(q, h, engine):
+            t = work.tile([P, 512, 4], BF16, tag="il", bufs=3, align_bytes=64, name="il")
+            interleave(engine, t[:], w_raw[q][:, :, h * 512 : h * 512 + 512])
+            il[("w", q, h)] = t
+
+        def w_quant(q, h):
+            cols = slice(h * 512, h * 512 + 512)
+            nc.vector.quantize_mx(out=w_codes[:, q, cols].bitcast(FP8X4), scales=w_scales[:, q, cols], in_=il[("w", q, h)][:].rearrange("p c t -> p (c t)"))
+
+        qt, stat, rb, rt, rq, o32, ac = {}, {}, {}, {}, {}, {}, {}
+
+        zt = {}
+
+        def logits(b, c):
+            z = psum.tile([P, CHUNK], F32, tag="z", bufs=4, name="z")
+            rows = slice(b * P, b * P + P)
+            cols = slice(c * CHUNK, c * CHUNK + CHUNK)
+            nc.tensor.matmul_mx(out=z[:], lhsT=h_codes[:, rows].bitcast(FP8X4), lhsT_scale=h_scales[:, rows], rhs=m_codes[:, cols].bitcast(FP8X4), rhs_scale=m_scales[:, cols], start=True, stop=False)
+            nc.tensor.matmul_mx(out=z[:], lhsT=k_codes[:, rows].bitcast(FP8X4), lhsT_scale=k_scales[:, rows], rhs=p_codes[:, cols].bitcast(FP8X4), rhs_scale=p_scales[:, cols], start=False, stop=True)
+            zt[(b, c)] = z
+
+        def addlp(b, c):
+            if c == 0:
+                qt[b] = work.tile([P, C], F32, tag="q", bufs=5, name="q")
+            cols = slice(c * CHUNK, c * CHUNK + CHUNK)
+            nc.vector.tensor_tensor(out=qt[b][:, cols], in0=zt[(b, c)][:], in1=lp_all[:, cols], op=ALU.add)
+
+        def rowmax(b):
+            nm = work.tile([P, 1], F32, tag="nm", bufs=4, name="nm")
+            nc.vector.tensor_reduce(out=nm[:], in_=qt[b][:], axis=AX.X, op=ALU.max, negate=True)
+            stat[b] = nm
+
+        def expo(b):
+            s = work.tile([P, 1], F32, tag="ssum", bufs=4, name="ssum")
+            nc.scalar.activation(out=qt[b][:], in_=qt[b][:], func=ACT.Exp, bias=stat[b][:], scale=1.0, accum_out=s[:])
+            stat[b] = s
+
+        def recip(b):
+            r = work.tile([P, 1], F32, tag="rs", bufs=4, name="rs")
+            nc.vector.reciprocal(out=r[:], in_=stat[b][:])
+            stat[b] = r
+
+        def norm(b):
+            for h in range(2):
+                cols = slice(h * 1024, h * 1024 + 1024)
+                if (b, h) in NORM_S:
+                    nc.scalar.activation(out=qt[b][:, cols], in_=qt[b][:, cols], func=ACT.Identity, bias=minus[:], scale=stat[b][:])
+                else:
+                    nc.gpsimd.tensor_scalar(out=qt[b][:, cols], in0=qt[b][:, cols], scalar1=stat[b][:], scalar2=-1.0 / C, op0=ALU.mult, op1=ALU.add)
+
+        def gain(b, h):
+            if h == 0:
+                rb[b] = work.tile([P, C], BF16, tag="rb", bufs=2, name="rb")
+            cols = slice(h * 1024, h * 1024 + 1024)
+            nc.vector.tensor_tensor(out=rb[b][:, cols], in0=qt[b][:, cols], in1=gc_all[:, cols], op=ALU.mult)
+
+        tp = {}
+
+        def turn(b, h):
+            if h == 0:
+                rt[b] = work.tile([P, PASSES, P, 4], BF16, tag="rt", bufs=2, align_bytes=64, name="rt")
+            words = rb[b][:].bitcast(F32)
+            ps = psum.tile([P, 2, 2, P], F32, tag="tr", bufs=2, name="rtp")
+            for s in range(2):
+                for u in range(2):
+                    w0 = 256 * (2 * h + s)
+                    nc.tensor.transpose(ps[:, s, u, :], words[:, w0 + u : w0 + 256 : 2], ident[:])
+            tp[(b, h)] = ps
+
+        def turned(b, h):
+            ps = tp[(b, h)]
+            nc.scalar.copy(out=rt[b][:, 2 * h : 2 * h + 2].bitcast(F32), in_=ps[:].rearrange("p s u r -> p s r u"))
+
+        def rquant(b, h):
+            if h == 0:
+                rq[b] = (work.tile([P, 512], U32, tag="rc", bufs=4, align_bytes=64, name="rc"), work.tile([P, 512], U8, tag="rsc", bufs=4, align_bytes=64, name="rsc"))
+            codes, scales = rq[b]
+            cols = slice(h * 256, h * 256 + 256)
+            nc.vector.quantize_mx(out=codes[:, cols].bitcast(FP8X4), scales=scales[:, cols], in_=rt[b][:, 2 * h : 2 * h + 2].rearrange("p q r t -> p (q r t)"))
+
+        def second(b):
+            g, t = divmod(b, 4)
+            codes, scales = rq[b]
+            acc = [psum.tile([P, 512], F32, tag="o", bufs=2, name="acc") for h in range(2)]
+            for h in range(2):
+                if (g, h) not in o32:
+                    o32[(g, h)] = work.tile([P, 4, 512], F32, tag="o32", bufs=3, name="o32")
+            for q in range(PASSES):
+                cols = slice(q * P, q * P + P)
+                for h in range(2):
+                    oc = slice(h * 512, h * 512 + 512)
+                    nc.tensor.matmul_mx(out=acc[h][:], lhsT=codes[:, cols].bitcast(FP8X4), lhsT_scale=scales[:, cols], rhs=w_codes[:, q, oc].bitcast(FP8X4), rhs_scale=w_scales[:, q, oc], start=(q == 0), stop=(q == PASSES - 1))
+            ac[b] = acc
+
+        def drain(b, h, engine="S"):
+            g, t = divmod(b, 4)
+            if engine == "S":
+                nc.scalar.copy(out=o32[(g, h)][:, t, :], in_=ac[b][h][:])
+            else:
+                nc.vector.tensor_copy(out=o32[(g, h)][:, t, :], in_=ac[b][h][:])
+            rows = out_0[g * 512 : g * 512 + 512, :].rearrange("(p t) o -> p t o", t=4)
+            nc.sync.dma_start(out=rows[:, t, h * 512 : h * 512 + 512], in_=o32[(g, h)][:, t, :])
+
+        def planes(g, h, engine):
+            ob = work.tile([P, 512, 4], BF16, tag="il", bufs=3, align_bytes=64, name="ob")
+            if engine == "VS":
+                interleave("V", ob[:, 0:256, :], o32[(g, h)][:, :, 0:256])
+                interleave("S", ob[:, 256:512, :], o32[(g, h)][:, :, 256:512])
+            else:
+                interleave(engine, ob[:], o32[(g, h)][:])
+            oc = work.tile([P, 512], U32, tag="oc", bufs=2, align_bytes=64, name="oc")
+            osc = work.tile([P, 512], U8, tag="osc", bufs=2, align_bytes=64, name="osc")
+            nc.vector.quantize_mx(out=oc[:].bitcast(FP8X4), scales=osc[:], in_=ob[:].rearrange("p c t -> p (c t)"))
+            cols = slice(h * 512, h * 512 + 512)
+            nc.sync.dma_start(out=out_1[g][:, cols, :].rearrange("p m t -> p (m t)").bitcast(I32), in_=oc[:].bitcast(I32))
+            for quad in range(4):
+                nc.sync.dma_start(out=out_2[g, 4 * quad : 4 * quad + 4, cols].bitcast(I32), in_=osc[32 * quad : 32 * quad + 4, :].bitcast(I32))
+
+        x1 = work.tile([P, 4, D], BF16, tag="x", bufs=2)
+        x_sb.append(x1)
+
+        def softmax(b):
+            rowmax(b)
+            expo(b)
+            recip(b)
+            norm(b)
+
+        prep_pair(0)
+        mp_inter("m", 0, "S")
+        mp_inter("p", 0, "V")
+        mp_quant("p", 0)
+        mp_quant("m", 0)
+        bcast(sel_lp, lp_all)
+        prep_pair(1)
+        bcast(sel_gc, gc_all)
+        nc.sync.dma_start(out=x1[:], in_=x_view[1])
+        w_load(0)
+        w_load(1)
+        for c in range(CHUNKS):
+            if c < 3:
+                mp_inter("m", c + 1, "S")
+                mp_inter("p", c + 1, "G")
+                mp_quant("m", c + 1)
+                mp_quant("p", c + 1)
+            for b in range(4):
+                logits(b, c)
+                addlp(b, c)
+                if c == 3 and b < 3:
+                    softmax(b)
+        prep_pair(2)
+        w_load(2)
+        w_load(3)
+        second_at = {2: (0,), 3: (1,2), 4: (3,), 5: (4,), 6: (5,), 7: (6,)}
+        for i in range(BLOCKS):
+            if i + 3 < BLOCKS:
+                softmax(i + 3)
+            for h in range(2):
+                gain(i, h)
+                turn(i, h)
+                turned(i, h)
+            for h in range(2):
+                rquant(i, h)
+            if i < 2:
+              for q in (2 * i, 2 * i + 1):
+                w_inter(q, 0, "S")
+                w_inter(q, 1, "G")
+                w_quant(q, 0)
+                w_quant(q, 1)
+            if i < 4:
+                for c in range(CHUNKS):
+                    logits(i + 4, c)
+                    addlp(i + 4, c)
+            for b in second_at.get(i, ()):
+                second(b)
+                drain(b, 0)
+                drain(b, 1)
+            if i == 0:
+                prep_pair(3)
+            if i == 5:
+                planes(0, 0, "S")
+            if i == 6:
+                planes(0, 1, "S")
+        second(7)
+        drain(7, 0, "S")
+        drain(7, 1, "V")
+        planes(1, 0, "VS")
+        planes(1, 1, "VS")

@@ -20,7 +20,14 @@ P = 128
 BLOCKS = N // P
 CHUNK = 512
 CHUNKS = C // CHUNK
-GSTEP = 256
+GSTEP = 128
+NSTEP = 512
+RAWB = 8
+ILB = 3
+QB = 6
+ZB, TB, OB = 3, 1, 2
+AG = {}
+GG = {(0, 1): 512, (1, 1): 512, (2, 1): 512, (3, 1): 512}
 NORM_S = ((6, 1), (7, 1))
 PASSES = C // 512
 
@@ -32,6 +39,7 @@ def tile_ellipticalnormalizedrbfnet_x1_kernel(tc, x, a, m, p, lp, gc, w, out_0, 
         keep = ctx.enter_context(tc.tile_pool(name="keep", bufs=1))
         work = ctx.enter_context(tc.tile_pool(name="work", bufs=2))
         psum = ctx.enter_context(tc.psum_pool(name="psum", bufs=2))
+        ctx.enter_context(tc.manual_schedule())
 
         h_codes = keep.tile([P, N], U32, align_bytes=64)
         h_scales = keep.tile([P, N], U8, align_bytes=64)
@@ -43,11 +51,12 @@ def tile_ellipticalnormalizedrbfnet_x1_kernel(tc, x, a, m, p, lp, gc, w, out_0, 
         p_scales = keep.tile([P, C], U8, align_bytes=64)
         w_codes = keep.tile([P, PASSES, O], U32, align_bytes=64)
         w_scales = keep.tile([P, PASSES, O], U8, align_bytes=64)
+        gc_all = const.tile([P, C], BF16)
         ident = const.tile([P, P], F32)
         sel_lp = const.tile([P, P], BF16)
         sel_gc = const.tile([P, P], BF16)
         lp_all = const.tile([P, C], BF16)
-        gc_all = const.tile([P, C], BF16)
+        gc_ps = [psum.tile([P, 1024], BF16, tag="gc", bufs=2, name="gcp") for gi in range(2)]
         a_col = const.tile([P, 4], BF16)
         a_neg = const.tile([P, 4], BF16)
         warm = const.tile([P, 1], F32)
@@ -64,7 +73,8 @@ def tile_ellipticalnormalizedrbfnet_x1_kernel(tc, x, a, m, p, lp, gc, w, out_0, 
 
         x_sb = []
         x0 = work.tile([P, 4, D], BF16, tag="x", bufs=2)
-        nc.sync.dma_start(out=x0[:], in_=x_view[0])
+        nc.sync.dma_start(out=x0[:, 0:2], in_=x_view[0][:, 0:2])
+        nc.sync.dma_start(out=x0[:, 2:4], in_=x_view[0][:, 2:4])
         x_sb.append(x0)
         nc.sync.dma_start(out=a_col[:], in_=a.rearrange("(p t) -> p t", t=4))
         vec = work.tile([P, C], BF16, tag="x", bufs=2)
@@ -72,15 +82,17 @@ def tile_ellipticalnormalizedrbfnet_x1_kernel(tc, x, a, m, p, lp, gc, w, out_0, 
         raw = {}
 
         def load_mp(name, view, lo, hi):
-            r = work.tile([P, 4, 512], BF16, tag="raw4", bufs=6, name="raw4")
-            nc.sync.dma_start(out=r[:], in_=view[:, :, lo:hi])
-            for s in range(lo, hi, 512):
-                raw[(name, s // 512)] = r[:, :, s - lo : s - lo + 512]
+            c = lo // 512
+            if c not in raw:
+                raw[c] = work.tile([P, 2, 4, 512], BF16, tag="raw", bufs=4, name="raw")
+            half = raw[c][:, 0 if name == "m" else 1]
+            nc.sync.dma_start(out=half, in_=view[:, :, lo:hi])
+            raw[(name, c)] = half
 
-        load_mp("m", m_view, 0, 512)
-        load_mp("p", p_view, 0, 512)
         nc.sync.dma_start(out=vec[0:1, :], in_=lp.unsqueeze(0))
         nc.sync.dma_start(out=vec[32:33, :], in_=gc.unsqueeze(0))
+        load_mp("m", m_view, 0, 512)
+        load_mp("p", p_view, 0, 512)
         for c in range(1, CHUNKS):
             load_mp("m", m_view, 512 * c, 512 * c + 512)
             load_mp("p", p_view, 512 * c, 512 * c + 512)
@@ -105,39 +117,66 @@ def tile_ellipticalnormalizedrbfnet_x1_kernel(tc, x, a, m, p, lp, gc, w, out_0, 
                 else:
                     nc.gpsimd.tensor_scalar(out=d, in0=s, scalar1=1.0, scalar2=0.0, op0=ALU.mult, op1=ALU.add)
 
-        def bcast(sel, dst):
+        lp_ps = {}
+
+        def spread_lp():
             for h in range(2):
-                ps = psum.tile([P, 1024], BF16, tag="o", bufs=2, name="bc")
+                ps = psum.tile([P, 1024], BF16, tag="z", bufs=ZB, name="bc")
                 for s in range(2):
                     c0 = h * 1024 + s * 512
-                    nc.tensor.matmul(ps[:, s * 512 : s * 512 + 512], lhsT=sel[:], rhs=vec[:, c0 : c0 + 512], start=True, stop=True)
-                nc.scalar.copy(out=dst[:, h * 1024 : h * 1024 + 1024], in_=ps[:])
+                    nc.tensor.matmul(ps[:, s * 512 : s * 512 + 512], lhsT=sel_lp[:], rhs=vec[:, c0 : c0 + 512], start=True, stop=True)
+                lp_ps[h] = ps
+
+        def lp_copy(h):
+            nc.scalar.copy(out=lp_all[:, h * 1024 : h * 1024 + 1024], in_=lp_ps[h][:])
+
+        def gc_copy(h):
+            nc.scalar.copy(out=gc_all[:, h * 1024 : h * 1024 + 1024], in_=gc_ps[h][:])
+
+        def spread_gc():
+            for h in range(2):
+                for s in range(2):
+                    c0 = h * 1024 + s * 512
+                    nc.tensor.matmul(gc_ps[h][:, s * 512 : s * 512 + 512], lhsT=sel_gc[:], rhs=vec[:, c0 : c0 + 512], start=True, stop=True)
 
         a3 = a_col[:].rearrange("p (u e) -> p u e", e=2).unsqueeze(1).to_broadcast([P, 256, 2, 2])
         n3 = a_neg[:].unsqueeze(1).to_broadcast([P, 256, 4])
 
-        def prep_pair(j):
+        xt, hb, kb, sqt = {}, {}, {}, {}
+
+        def x_turn(j):
             g, t0 = divmod(2 * j, 4)
             words = x_sb[g][:].bitcast(F32)
-            ps = psum.tile([P, 2, 256], F32, tag="tr", bufs=2, name="xt")
+            ps = psum.tile([P, 2, 256], F32, tag="o", bufs=OB, name="xt")
             for b in range(2):
                 for u in range(2):
                     nc.tensor.transpose(ps[:, u, b * P : b * P + P], words[:, t0 + b, u : 256 : 2], ident[:])
-            xt = ps[:].bitcast(BF16).rearrange("p u (r e) -> p r u e", e=2)
-            hb = work.tile([P, 256, 4], BF16, tag="hb", bufs=2, align_bytes=64, name="hb")
-            kb = work.tile([P, 256, 4], BF16, tag="kb", bufs=2, align_bytes=64, name="kb")
-            sq = work.tile([P, 256, 4], F32, tag="sq", bufs=1, name="sq")
-            nc.scalar.activation(out=sq[:].rearrange("p r (u e) -> p r u e", e=2), in_=xt, func=ACT.Square)
-            nc.vector.tensor_tensor(out=hb[:].rearrange("p r (u e) -> p r u e", e=2), in0=xt, in1=a3, op=ALU.mult)
-            nc.vector.scalar_tensor_tensor(out=kb[:], in0=sq[:], scalar=1.0, in1=n3, op0=ALU.subtract, op1=ALU.mult)
+            xt[j] = ps[:].bitcast(BF16).rearrange("p u (r e) -> p r u e", e=2)
+
+        def x_square(j):
+            sqt[j] = work.tile([P, 256, 4], F32, tag="sq", bufs=2, name="sq")
+            nc.scalar.activation(out=sqt[j][:].rearrange("p r (u e) -> p r u e", e=2), in_=xt[j], func=ACT.Square)
+
+        def x_h(j):
+            hb[j] = work.tile([P, 256, 4], BF16, tag="hb", bufs=2, align_bytes=64, name="hb")
+            nc.vector.tensor_tensor(out=hb[j][:].rearrange("p r (u e) -> p r u e", e=2), in0=xt[j], in1=a3, op=ALU.mult)
+
+        def x_k(j):
+            kb[j] = work.tile([P, 256, 4], BF16, tag="kb", bufs=2, align_bytes=64, name="kb")
+            nc.vector.scalar_tensor_tensor(out=kb[j][:], in0=sqt[j][:], scalar=1.0, in1=n3, op0=ALU.subtract, op1=ALU.mult)
+
+        def h_quant(j):
             cols = slice(j * 256, j * 256 + 256)
-            nc.vector.quantize_mx(out=h_codes[:, cols].bitcast(FP8X4), scales=h_scales[:, cols], in_=hb[:].rearrange("p r t -> p (r t)"))
-            nc.vector.quantize_mx(out=k_codes[:, cols].bitcast(FP8X4), scales=k_scales[:, cols], in_=kb[:].rearrange("p r t -> p (r t)"))
+            nc.vector.quantize_mx(out=h_codes[:, cols].bitcast(FP8X4), scales=h_scales[:, cols], in_=hb[j][:].rearrange("p r t -> p (r t)"))
+
+        def k_quant(j):
+            cols = slice(j * 256, j * 256 + 256)
+            nc.vector.quantize_mx(out=k_codes[:, cols].bitcast(FP8X4), scales=k_scales[:, cols], in_=kb[j][:].rearrange("p r t -> p (r t)"))
 
         il = {}
 
         def mp_inter(name, c, engine):
-            t = work.tile([P, 512, 4], BF16, tag="il", bufs=3, align_bytes=64, name="il")
+            t = work.tile([P, 512, 4], BF16, tag="ob" if engine == "V" else "il" + engine, bufs=2 if engine == "V" else ILB, align_bytes=64, name="il")
             interleave(engine, t[:], raw[(name, c)])
             il[(name, c)] = t
 
@@ -149,13 +188,14 @@ def tile_ellipticalnormalizedrbfnet_x1_kernel(tc, x, a, m, p, lp, gc, w, out_0, 
         w_raw = {}
 
         def w_load(q):
-            r = work.tile([P, 4, 1024], BF16, tag="raw8", bufs=2, name="raw8")
+            r = work.tile([P, 4, 1024], BF16, tag="raw", bufs=4, name="raw")
             nc.sync.dma_start(out=r[:], in_=w_view[q])
-            w_raw[q] = r
+            for h in range(2):
+                w_raw[(q, h)] = r[:, :, h * 512 : h * 512 + 512]
 
         def w_inter(q, h, engine):
-            t = work.tile([P, 512, 4], BF16, tag="il", bufs=3, align_bytes=64, name="il")
-            interleave(engine, t[:], w_raw[q][:, :, h * 512 : h * 512 + 512])
+            t = work.tile([P, 512, 4], BF16, tag="il" + engine, bufs=ILB, align_bytes=64, name="il")
+            interleave(engine, t[:], w_raw[(q, h)])
             il[("w", q, h)] = t
 
         def w_quant(q, h):
@@ -167,7 +207,7 @@ def tile_ellipticalnormalizedrbfnet_x1_kernel(tc, x, a, m, p, lp, gc, w, out_0, 
         zt = {}
 
         def logits(b, c):
-            z = psum.tile([P, CHUNK], F32, tag="z", bufs=4, name="z")
+            z = psum.tile([P, CHUNK], F32, tag="z", bufs=ZB, name="z")
             rows = slice(b * P, b * P + P)
             cols = slice(c * CHUNK, c * CHUNK + CHUNK)
             nc.tensor.matmul_mx(out=z[:], lhsT=h_codes[:, rows].bitcast(FP8X4), lhsT_scale=h_scales[:, rows], rhs=m_codes[:, cols].bitcast(FP8X4), rhs_scale=m_scales[:, cols], start=True, stop=False)
@@ -175,8 +215,8 @@ def tile_ellipticalnormalizedrbfnet_x1_kernel(tc, x, a, m, p, lp, gc, w, out_0, 
             zt[(b, c)] = z
 
         def addlp(b, c):
-            if c == 0:
-                qt[b] = work.tile([P, C], F32, tag="q", bufs=5, name="q")
+            if b not in qt:
+                qt[b] = work.tile([P, C], F32, tag="q", bufs=6, name="q")
             cols = slice(c * CHUNK, c * CHUNK + CHUNK)
             nc.vector.tensor_tensor(out=qt[b][:, cols], in0=zt[(b, c)][:], in1=lp_all[:, cols], op=ALU.add)
 
@@ -195,27 +235,36 @@ def tile_ellipticalnormalizedrbfnet_x1_kernel(tc, x, a, m, p, lp, gc, w, out_0, 
             nc.vector.reciprocal(out=r[:], in_=stat[b][:])
             stat[b] = r
 
-        def norm(b):
-            for h in range(2):
-                cols = slice(h * 1024, h * 1024 + 1024)
-                if (b, h) in NORM_S:
-                    nc.scalar.activation(out=qt[b][:, cols], in_=qt[b][:, cols], func=ACT.Identity, bias=minus[:], scale=stat[b][:])
-                else:
+        def norm(b, h, engine):
+            cols = slice(0, C)
+            if engine == "S":
+                nc.scalar.activation(out=qt[b][:, cols], in_=qt[b][:, cols], func=ACT.Identity, bias=minus[:], scale=stat[b][:])
+            else:
+                for c0 in range(0, C, NSTEP):
+                    cols = slice(c0, c0 + NSTEP)
                     nc.gpsimd.tensor_scalar(out=qt[b][:, cols], in0=qt[b][:, cols], scalar1=stat[b][:], scalar2=-1.0 / C, op0=ALU.mult, op1=ALU.add)
 
         def gain(b, h):
-            if h == 0:
+            if b not in rb:
                 rb[b] = work.tile([P, C], BF16, tag="rb", bufs=2, name="rb")
-            cols = slice(h * 1024, h * 1024 + 1024)
-            nc.vector.tensor_tensor(out=rb[b][:, cols], in0=qt[b][:, cols], in1=gc_all[:, cols], op=ALU.mult)
+            lo = h * 1024
+            mid = lo + 1024 - GG.get((b, h), 0)
+            nc.vector.tensor_tensor(out=rb[b][:, lo:mid], in0=qt[b][:, lo:mid], in1=gc_ps[h][:, 0 : mid - lo], op=ALU.mult)
+
+        def gain_g(b, h):
+            if b not in rb:
+                rb[b] = work.tile([P, C], BF16, tag="rb", bufs=2, name="rb")
+            hi = h * 1024 + 1024
+            mid = hi - GG[(b, h)]
+            nc.gpsimd.tensor_tensor(out=rb[b][:, mid:hi], in0=qt[b][:, mid:hi], in1=gc_all[:, mid:hi], op=ALU.mult)
 
         tp = {}
 
         def turn(b, h):
-            if h == 0:
+            if b not in rt:
                 rt[b] = work.tile([P, PASSES, P, 4], BF16, tag="rt", bufs=2, align_bytes=64, name="rt")
             words = rb[b][:].bitcast(F32)
-            ps = psum.tile([P, 2, 2, P], F32, tag="tr", bufs=2, name="rtp")
+            ps = psum.tile([P, 2, 2, P], F32, tag="tr", bufs=TB, name="rtp")
             for s in range(2):
                 for u in range(2):
                     w0 = 256 * (2 * h + s)
@@ -227,116 +276,346 @@ def tile_ellipticalnormalizedrbfnet_x1_kernel(tc, x, a, m, p, lp, gc, w, out_0, 
             nc.scalar.copy(out=rt[b][:, 2 * h : 2 * h + 2].bitcast(F32), in_=ps[:].rearrange("p s u r -> p s r u"))
 
         def rquant(b, h):
-            if h == 0:
+            if b not in rq:
                 rq[b] = (work.tile([P, 512], U32, tag="rc", bufs=4, align_bytes=64, name="rc"), work.tile([P, 512], U8, tag="rsc", bufs=4, align_bytes=64, name="rsc"))
             codes, scales = rq[b]
             cols = slice(h * 256, h * 256 + 256)
             nc.vector.quantize_mx(out=codes[:, cols].bitcast(FP8X4), scales=scales[:, cols], in_=rt[b][:, 2 * h : 2 * h + 2].rearrange("p q r t -> p (q r t)"))
 
-        def second(b):
+        def second(b, h):
             g, t = divmod(b, 4)
             codes, scales = rq[b]
-            acc = [psum.tile([P, 512], F32, tag="o", bufs=2, name="acc") for h in range(2)]
-            for h in range(2):
-                if (g, h) not in o32:
-                    o32[(g, h)] = work.tile([P, 4, 512], F32, tag="o32", bufs=3, name="o32")
+            acc = psum.tile([P, 512], F32, tag="o", bufs=OB, name="acc")
+            ac[(b, h)] = acc
+            oc = slice(h * 512, h * 512 + 512)
             for q in range(PASSES):
                 cols = slice(q * P, q * P + P)
-                for h in range(2):
-                    oc = slice(h * 512, h * 512 + 512)
-                    nc.tensor.matmul_mx(out=acc[h][:], lhsT=codes[:, cols].bitcast(FP8X4), lhsT_scale=scales[:, cols], rhs=w_codes[:, q, oc].bitcast(FP8X4), rhs_scale=w_scales[:, q, oc], start=(q == 0), stop=(q == PASSES - 1))
-            ac[b] = acc
+                nc.tensor.matmul_mx(out=acc[:], lhsT=codes[:, cols].bitcast(FP8X4), lhsT_scale=scales[:, cols], rhs=w_codes[:, q, oc].bitcast(FP8X4), rhs_scale=w_scales[:, q, oc], start=(q == 0), stop=(q == PASSES - 1))
 
         def drain(b, h, engine="S"):
             g, t = divmod(b, 4)
+            if (g, h) not in o32:
+                o32[(g, h)] = work.tile([P, 4, 512], F32, tag="raw", bufs=4, name="o32")
             if engine == "S":
-                nc.scalar.copy(out=o32[(g, h)][:, t, :], in_=ac[b][h][:])
+                nc.scalar.copy(out=o32[(g, h)][:, t, :], in_=ac[(b, h)][:])
             else:
-                nc.vector.tensor_copy(out=o32[(g, h)][:, t, :], in_=ac[b][h][:])
+                nc.vector.tensor_copy(out=o32[(g, h)][:, t, :], in_=ac[(b, h)][:])
             rows = out_0[g * 512 : g * 512 + 512, :].rearrange("(p t) o -> p t o", t=4)
             nc.sync.dma_start(out=rows[:, t, h * 512 : h * 512 + 512], in_=o32[(g, h)][:, t, :])
 
-        def planes(g, h, engine):
-            ob = work.tile([P, 512, 4], BF16, tag="il", bufs=3, align_bytes=64, name="ob")
-            if engine == "VS":
-                interleave("V", ob[:, 0:256, :], o32[(g, h)][:, :, 0:256])
-                interleave("S", ob[:, 256:512, :], o32[(g, h)][:, :, 256:512])
-            else:
-                interleave(engine, ob[:], o32[(g, h)][:])
+        obt = {}
+
+        def o_inter(g, h, engine, lo=0, hi=512):
+            if (g, h) not in obt:
+                ob = work.tile([P, 512, 4], BF16, tag="ob", bufs=2, align_bytes=64, name="ob")
+                obt[(g, h)] = ob
+            interleave(engine, obt[(g, h)][:, lo:hi, :], o32[(g, h)][:, :, lo:hi])
+
+        def o_quant(g, h):
+            ob = obt[(g, h)]
             oc = work.tile([P, 512], U32, tag="oc", bufs=2, align_bytes=64, name="oc")
-            osc = work.tile([P, 512], U8, tag="osc", bufs=2, align_bytes=64, name="osc")
+            osc = work.tile([P, 512], U8, tag="os", bufs=2, align_bytes=64, name="os")
             nc.vector.quantize_mx(out=oc[:].bitcast(FP8X4), scales=osc[:], in_=ob[:].rearrange("p c t -> p (c t)"))
             cols = slice(h * 512, h * 512 + 512)
             nc.sync.dma_start(out=out_1[g][:, cols, :].rearrange("p m t -> p (m t)").bitcast(I32), in_=oc[:].bitcast(I32))
             for quad in range(4):
                 nc.sync.dma_start(out=out_2[g, 4 * quad : 4 * quad + 4, cols].bitcast(I32), in_=osc[32 * quad : 32 * quad + 4, :].bitcast(I32))
 
+
         x1 = work.tile([P, 4, D], BF16, tag="x", bufs=2)
         x_sb.append(x1)
+        load_q, tensor_q, scalar_q, gpsimd_q, vector_q = [], [], [], [], []
 
-        def softmax(b):
-            rowmax(b)
-            expo(b)
-            recip(b)
-            norm(b)
+        def put(queue, name, call, *needs):
+            queue.append((name, needs, call))
 
-        prep_pair(0)
-        mp_inter("m", 0, "S")
-        mp_inter("p", 0, "V")
-        mp_quant("p", 0)
-        mp_quant("m", 0)
-        bcast(sel_lp, lp_all)
-        prep_pair(1)
-        bcast(sel_gc, gc_all)
-        nc.sync.dma_start(out=x1[:], in_=x_view[1])
-        w_load(0)
-        w_load(1)
+        def T(name, call, *needs):
+            put(tensor_q, name, call, *needs)
+
+        def S(name, call, *needs):
+            put(scalar_q, name, call, *needs)
+
+        def G(name, call, *needs):
+            put(gpsimd_q, name, call, *needs)
+
+        def V(name, call, *needs):
+            put(vector_q, name, call, *needs)
+
+        put(load_q, "x1", lambda: nc.sync.dma_start(out=x1[:], in_=x_view[1]), ("xt", 0), ("xt", 1))
+        for q in range(PASSES):
+            put(load_q, ("wl", q), lambda q=q: w_load(q), ("I", "m", q), ("I", "p", q))
+
+        def t_xt(j):
+            T(("xt", j), lambda: x_turn(j), *(["x1"] if j >= 2 else []), *([("sq", j - 2), ("h", j - 2)] if j >= 2 else []))
+
+        def t_z(b, c):
+            T(("z", b, c), lambda: logits(b, c), ("qh", b // 2), ("qk", b // 2), ("Q", "m", c), ("Q", "p", c))
+
+        def t_turn(b, h):
+            T(("t", b, h), lambda: turn(b, h), *([("d", b, h)] if GG.get((b, h), 0) < 1024 else []), *([("dg", b, h)] if (b, h) in GG else []))
+
+        def t_second(b, h):
+            T(("o", b, h), lambda: second(b, h), ("qr", b, 0), ("qr", b, 1), *[("Qw", q, h) for q in range(PASSES)])
+
+        def s_sq(j):
+            S(("sq", j), lambda: x_square(j), ("xt", j))
+
+        def inter_mp(fn, engine, name, c):
+            fn(("I", name, c), lambda: mp_inter(name, c, engine))
+
+        def inter_w(fn, engine, q, h):
+            fn(("iw", q, h), lambda: w_inter(q, h, engine), ("wl", q))
+
+        def s_exp(b):
+            S(("e", b), lambda: expo(b), ("m", b))
+
+        def s_turned(b, h):
+            S(("tc", b, h), lambda: turned(b, h), ("t", b, h))
+
+        def s_drain(b, h):
+            S(("dr", b, h), lambda: drain(b, h), ("o", b, h))
+
+        def inter_o(fn, engine, g, h, lo=0, hi=512):
+            fn(("io", g, h, lo), lambda: o_inter(g, h, engine, lo, hi), *[("dr", 4 * g + t, h) for t in range(4)])
+
+        def norms(fn, engine, b, h):
+            fn(("n", b, h), lambda: norm(b, h, engine), ("r", b))
+
+        def g_gain(b, h):
+            G(("dg", b, h), lambda: gain_g(b, h), ("n", b, 0), "gccopy")
+
+        def v_h(j):
+            V(("h", j), lambda: x_h(j), ("xt", j))
+
+        def v_k(j):
+            V(("k", j), lambda: x_k(j), ("sq", j))
+
+        def v_qh(j):
+            V(("qh", j), lambda: h_quant(j), ("h", j))
+
+        def v_qk(j):
+            V(("qk", j), lambda: k_quant(j), ("k", j))
+
+        def v_q(name, c):
+            V(("Q", name, c), lambda: mp_quant(name, c), ("I", name, c))
+
+        def v_a(b, c):
+            V(("a", b, c), lambda: addlp(b, c), ("z", b, c), "lp0" if c < 2 else "lp1")
+
+        def v_max(b):
+            V(("m", b), lambda: rowmax(b), *[("a", b, c) for c in range(CHUNKS)])
+
+        def v_recip(b):
+            V(("r", b), lambda: recip(b), ("e", b))
+
+        def v_gain(b, h):
+            V(("d", b, h), lambda: gain(b, h), ("n", b, 0), "gcps")
+
+        def v_qr(b, h):
+            V(("qr", b, h), lambda: rquant(b, h), ("tc", b, h))
+
+        def v_qw(q, h):
+            V(("Qw", q, h), lambda: w_quant(q, h), ("iw", q, h))
+
+        def v_qo(g, h, *los):
+            V(("qo", g, h), lambda: o_quant(g, h), *[("io", g, h, lo) for lo in los])
+
+        LAG = 4
+        t_xt(0)
+        t_xt(1)
+        T("lpps", spread_lp)
         for c in range(CHUNKS):
-            if c < 3:
-                mp_inter("m", c + 1, "S")
-                mp_inter("p", c + 1, "G")
-                mp_quant("m", c + 1)
-                mp_quant("p", c + 1)
             for b in range(4):
-                logits(b, c)
-                addlp(b, c)
-                if c == 3 and b < 3:
-                    softmax(b)
-        prep_pair(2)
-        w_load(2)
-        w_load(3)
-        second_at = {2: (0,), 3: (1,2), 4: (3,), 5: (4,), 6: (5,), 7: (6,)}
-        for i in range(BLOCKS):
-            if i + 3 < BLOCKS:
-                softmax(i + 3)
-            for h in range(2):
-                gain(i, h)
-                turn(i, h)
-                turned(i, h)
-            for h in range(2):
-                rquant(i, h)
-            if i < 2:
-              for q in (2 * i, 2 * i + 1):
-                w_inter(q, 0, "S")
-                w_inter(q, 1, "G")
-                w_quant(q, 0)
-                w_quant(q, 1)
-            if i < 4:
-                for c in range(CHUNKS):
-                    logits(i + 4, c)
-                    addlp(i + 4, c)
-            for b in second_at.get(i, ()):
-                second(b)
-                drain(b, 0)
-                drain(b, 1)
+                t_z(b, c)
+            if c == 1:
+                t_xt(2)
+            if c == 2:
+                T("gcps", spread_gc)
+                t_xt(3)
+        for i in range(BLOCKS + 2):
+            n = i + LAG
+            if n < BLOCKS:
+                t_z(n, 0)
+                t_z(n, 1)
+                t_z(n, 2)
+            if i >= 2:
+                t_second(i - 2, 0)
+            if i < BLOCKS:
+                t_turn(i, 0)
+            if n < BLOCKS:
+                t_z(n, 3)
+            if i >= 2:
+                t_second(i - 2, 1)
+            if i < BLOCKS:
+                t_turn(i, 1)
+
+        s_sq(0)
+        s_sq(1)
+        inter_mp(S, "S", "m", 0)
+        S("lp0", lambda: lp_copy(0), "lpps")
+        S("lp1", lambda: lp_copy(1), "lpps")
+        inter_mp(S, "S", "m", 1)
+        inter_mp(S, "S", "p", 1)
+        inter_mp(S, "S", "p", 2)
+        inter_mp(S, "S", "m", 2)
+        s_sq(2)
+        inter_mp(S, "S", "m", 3)
+        inter_w(S, "S", 0, 0)
+        s_sq(3)
+        inter_w(S, "S", 0, 1)
+        inter_w(S, "S", 1, 0)
+        s_exp(0)
+        S("gccopy", lambda: (gc_copy(0), gc_copy(1)), "gcps")
+        inter_w(S, "S", 1, 1)
+        s_exp(1)
+        inter_w(S, "S", 2, 0)
+        s_exp(2)
+        s_exp(3)
+        for i in range(BLOCKS + 2):
+            if i < BLOCKS:
+                s_turned(i, 0)
+            if i >= 2:
+                s_drain(i - 2, 0)
+                if i < BLOCKS + 1:
+                    s_drain(i - 2, 1)
+            if i < BLOCKS:
+                s_turned(i, 1)
             if i == 0:
-                prep_pair(3)
-            if i == 5:
-                planes(0, 0, "S")
-            if i == 6:
-                planes(0, 1, "S")
-        second(7)
-        drain(7, 0, "S")
-        drain(7, 1, "V")
-        planes(1, 0, "VS")
-        planes(1, 1, "VS")
+                inter_w(S, "S", 2, 1)
+            if i + LAG < BLOCKS:
+                s_exp(i + LAG)
+        inter_o(S, "S", 1, 0, 320, 512)
+        inter_o(S, "S", 1, 1, 320, 512)
+
+        inter_mp(G, "G", "p", 3)
+        for b in range(BLOCKS):
+            norms(G, "G", b, 0)
+            if (b, 1) in GG:
+                g_gain(b, 1)
+            if b < 2:
+                inter_w(G, "G", 3, b)
+        inter_o(G, "G", 0, 1)
+
+        v_h(0)
+        v_h(1)
+        v_qh(0)
+        v_qh(1)
+        V(("I", "p", 0), lambda: mp_inter("p", 0, "V"))
+        v_k(0)
+        v_k(1)
+        v_qk(0)
+        v_qk(1)
+        v_q("p", 0)
+        v_q("m", 0)
+        for b in range(4):
+            v_a(b, 0)
+        v_q("m", 1)
+        v_q("p", 1)
+        for b in range(4):
+            v_a(b, 1)
+        v_h(2)
+        v_q("p", 2)
+        v_q("m", 2)
+        v_k(2)
+        for b in range(4):
+            v_a(b, 2)
+        v_qh(2)
+        v_q("m", 3)
+        v_q("p", 3)
+        v_a(0, 3)
+        v_a(1, 3)
+        v_h(3)
+        v_max(0)
+        v_a(2, 3)
+        v_a(3, 3)
+        v_qk(2)
+        v_k(3)
+        v_qh(3)
+        v_max(1)
+        v_qw(0, 0)
+        v_qw(0, 1)
+        v_recip(0)
+        v_max(2)
+        v_qk(3)
+        v_qw(1, 0)
+        v_recip(1)
+        v_max(3)
+        late_w = {0: ((1, 1), (2, 0)), 1: ((3, 0), (2, 1), (3, 1))}
+        for i in range(BLOCKS):
+            n = i + LAG
+            v_gain(i, 0)
+            if n < BLOCKS:
+                v_a(n, 0)
+                v_a(n, 1)
+            if i < 6:
+                v_recip(i + 2)
+            v_gain(i, 1)
+            if n < BLOCKS:
+                v_a(n, 2)
+                v_a(n, 3)
+            if i >= 1:
+                v_qr(i - 1, 0)
+                v_qr(i - 1, 1)
+            for q, h in late_w.get(i, ()):
+                v_qw(q, h)
+            if n < BLOCKS:
+                v_max(n)
+        v_qr(7, 0)
+        v_qr(7, 1)
+        inter_o(V, "V", 0, 0)
+        v_qo(0, 0, 0)
+        v_qo(0, 1, 0)
+        inter_o(V, "V", 1, 0, 0, 320)
+        V(("dr", 7, 1), lambda: drain(7, 1, "V"), ("o", 7, 1))
+        inter_o(V, "V", 1, 1, 0, 320)
+        v_qo(1, 0, 0, 320)
+        v_qo(1, 1, 0, 320)
+
+
+        def ring(seq, n, freed_by):
+            for later, earlier in zip(seq[n:], seq):
+                extra.setdefault(later, []).extend(freed_by(earlier))
+
+        extra = {}
+        t_order = [task[0] for task in tensor_q]
+        s_order = [task[0] for task in scalar_q]
+        g_order = [task[0] for task in gpsimd_q]
+        v_order = [task[0] for task in vector_q]
+        ring([k for k in t_order if k[0] == "z"], ZB, lambda k: [("a",) + k[1:]])
+        extra.setdefault([k for k in t_order if k[0] == "z"][ZB - 2], []).extend(["lp0", "lp1"])
+        ring([k for k in t_order if k[0] == "t"], TB, lambda k: [("tc",) + k[1:]])
+        ring([k for k in t_order if k[0] == "o"], OB, lambda k: [("dr",) + k[1:]])
+        for k in [k for k in t_order if k[0] == "o"][:2]:
+            extra.setdefault(k, []).extend([("sq", 2), ("sq", 3), ("h", 2), ("h", 3)])
+        for order in (s_order, g_order):
+            ring([k for k in order if k[0] in ("I", "iw")], ILB, lambda k: [("Q",) + k[1:]] if k[0] == "I" else [("Qw",) + k[1:]])
+        ring([k for k in s_order if k[0] == "sq"], 2, lambda k: [("k", k[1])])
+        ring([k for k in v_order if k[0] == "h"], 2, lambda k: [("qh", k[1])])
+        ring([k for k in v_order if k[0] == "k"], 2, lambda k: [("qk", k[1])])
+        for b in range(2, BLOCKS):
+            for h in range(2):
+                extra.setdefault(("d", b, h), []).extend([("t", b - 2, 0), ("t", b - 2, 1)])
+                extra.setdefault(("dg", b, h), []).extend([("t", b - 2, 0), ("t", b - 2, 1)])
+                extra.setdefault(("t", b, h), []).extend([("qr", b - 2, 0), ("qr", b - 2, 1)])
+                if b >= 4:
+                    extra.setdefault(("qr", b, h), []).extend([("o", b - 4, 0), ("o", b - 4, 1)])
+            if b >= 4:
+                extra.setdefault(("m", b), []).append(("e", b - 4))
+                extra.setdefault(("e", b), []).append(("r", b - 4))
+                extra.setdefault(("r", b), []).append(("n", b - 4, 0))
+            if b >= QB:
+                for c in range(CHUNKS):
+                    extra.setdefault(("a", b, c), []).extend([k for k in v_order + g_order if k[0] in ("d", "dg") and k[1] == b - QB])
+        for h in range(2):
+            for lo in (0, 320):
+                extra[("io", 1, h, lo)] = [("qo", 0, h)]
+        done = set()
+        queues = [load_q, tensor_q, scalar_q, gpsimd_q, vector_q]
+        while any(queues):
+            before = len(done)
+            for queue in queues:
+                while queue and all(need in done for need in (*queue[0][1], *extra.get(queue[0][0], []))):
+                    name, needs, call = queue.pop(0)
+                    call()
+                    done.add(name)
+            assert len(done) > before, [q[0][:2] for q in queues if q]

from contextlib import ExitStack

import concourse.mybir as mybir
from concourse.masks import make_identity

N, D, C, O = 1024, 512, 2048, 1024
FLOPS = 2 * N * D * C * 2 + 2 * N * C * O

F32 = mybir.dt.float32
BF16 = mybir.dt.bfloat16
U32 = mybir.dt.uint32
I32 = mybir.dt.int32
U8 = mybir.dt.uint8
FP8X4 = mybir.dt.float8_e4m3fn_x4
ALU = mybir.AluOpType
ACT = mybir.ActivationFunctionType
AX = mybir.AxisListType

P = 128
BLOCKS = N // P
CHUNK = 512
CHUNKS = C // CHUNK
GSTEP = 128
NSTEP = 512
RAWB = 8
ILB = 3
QB = 6
ZB, TB, OB = 3, 1, 2
AG = {}
GG = {(0, 1): 512, (1, 1): 512, (2, 1): 512, (3, 1): 512}
NORM_S = ((6, 1), (7, 1))
PASSES = C // 512


def tile_ellipticalnormalizedrbfnet_x1_kernel(tc, x, a, m, p, lp, gc, w, out_0, out_1, out_2):
    nc = tc.nc
    with ExitStack() as ctx:
        const = ctx.enter_context(tc.tile_pool(name="const", bufs=1))
        keep = ctx.enter_context(tc.tile_pool(name="keep", bufs=1))
        work = ctx.enter_context(tc.tile_pool(name="work", bufs=2))
        psum = ctx.enter_context(tc.psum_pool(name="psum", bufs=2))
        ctx.enter_context(tc.manual_schedule())

        h_codes = keep.tile([P, N], U32, align_bytes=64)
        h_scales = keep.tile([P, N], U8, align_bytes=64)
        k_codes = keep.tile([P, N], U32, align_bytes=64)
        k_scales = keep.tile([P, N], U8, align_bytes=64)
        m_codes = keep.tile([P, C], U32, align_bytes=64)
        m_scales = keep.tile([P, C], U8, align_bytes=64)
        p_codes = keep.tile([P, C], U32, align_bytes=64)
        p_scales = keep.tile([P, C], U8, align_bytes=64)
        w_codes = keep.tile([P, PASSES, O], U32, align_bytes=64)
        w_scales = keep.tile([P, PASSES, O], U8, align_bytes=64)
        gc_all = const.tile([P, C], BF16)
        ident = const.tile([P, P], F32)
        sel_lp = const.tile([P, P], BF16)
        sel_gc = const.tile([P, P], BF16)
        lp_all = const.tile([P, C], BF16)
        gc_ps = [psum.tile([P, 1024], BF16, tag="gc", bufs=2, name="gcp") for gi in range(2)]
        a_col = const.tile([P, 4], BF16)
        a_neg = const.tile([P, 4], BF16)
        warm = const.tile([P, 1], F32)
        minus = const.tile([P, 1], F32)

        x_view = x.rearrange("(g p t) d -> g p t d", g=2, t=4)
        m_view = m.rearrange("(p j) c -> p j c", j=4)
        p_view = p.rearrange("(p j) c -> p j c", j=4)
        w_view = w.rearrange("(q p j) o -> q p j o", q=PASSES, j=4)

        nc.vector.memset(warm[:], 0.0)
        nc.vector.memset(minus[:], -1.0 / C)
        nc.scalar.activation(out=warm[:], in_=warm[:], func=ACT.Exp)

        x_sb = []
        x0 = work.tile([P, 4, D], BF16, tag="x", bufs=2)
        nc.sync.dma_start(out=x0[:, 0:2], in_=x_view[0][:, 0:2])
        nc.sync.dma_start(out=x0[:, 2:4], in_=x_view[0][:, 2:4])
        x_sb.append(x0)
        nc.sync.dma_start(out=a_col[:], in_=a.rearrange("(p t) -> p t", t=4))
        vec = work.tile([P, C], BF16, tag="x", bufs=2)
        nc.vector.memset(vec[:], 0.0)
        raw = {}

        def load_mp(name, view, lo, hi):
            c = lo // 512
            if c not in raw:
                raw[c] = work.tile([P, 2, 4, 512], BF16, tag="raw", bufs=4, name="raw")
            half = raw[c][:, 0 if name == "m" else 1]
            nc.sync.dma_start(out=half, in_=view[:, :, lo:hi])
            raw[(name, c)] = half

        nc.sync.dma_start(out=vec[0:1, :], in_=lp.unsqueeze(0))
        nc.sync.dma_start(out=vec[32:33, :], in_=gc.unsqueeze(0))
        load_mp("m", m_view, 0, 512)
        load_mp("p", p_view, 0, 512)
        for c in range(1, CHUNKS):
            load_mp("m", m_view, 512 * c, 512 * c + 512)
            load_mp("p", p_view, 512 * c, 512 * c + 512)

        make_identity(nc, ident[:])
        nc.gpsimd.memset(sel_lp[:], 0.0)
        nc.gpsimd.memset(sel_lp[0:1, :], 1.0)
        nc.gpsimd.memset(sel_gc[:], 0.0)
        nc.gpsimd.memset(sel_gc[32:33, :], float(C))
        nc.vector.tensor_scalar_mul(a_neg[:], a_col[:], -1.0)

        def interleave(engine, dst, src):
            n = dst.shape[1]
            step = GSTEP if engine == "G" else n
            for c0 in range(0, n, step):
                d = dst[:, c0 : c0 + step].rearrange("p (c i) t -> p c t i", i=4)
                s = src[:, :, c0 : c0 + step].rearrange("p t (c i) -> p c t i", i=4)
                if engine == "V":
                    nc.vector.tensor_copy(out=d, in_=s)
                elif engine == "S":
                    nc.scalar.copy(out=d, in_=s)
                else:
                    nc.gpsimd.tensor_scalar(out=d, in0=s, scalar1=1.0, scalar2=0.0, op0=ALU.mult, op1=ALU.add)

        lp_ps = {}

        def spread_lp():
            for h in range(2):
                ps = psum.tile([P, 1024], BF16, tag="z", bufs=ZB, name="bc")
                for s in range(2):
                    c0 = h * 1024 + s * 512
                    nc.tensor.matmul(ps[:, s * 512 : s * 512 + 512], lhsT=sel_lp[:], rhs=vec[:, c0 : c0 + 512], start=True, stop=True)
                lp_ps[h] = ps

        def lp_copy(h):
            nc.scalar.copy(out=lp_all[:, h * 1024 : h * 1024 + 1024], in_=lp_ps[h][:])

        def gc_copy(h):
            nc.scalar.copy(out=gc_all[:, h * 1024 : h * 1024 + 1024], in_=gc_ps[h][:])

        def spread_gc():
            for h in range(2):
                for s in range(2):
                    c0 = h * 1024 + s * 512
                    nc.tensor.matmul(gc_ps[h][:, s * 512 : s * 512 + 512], lhsT=sel_gc[:], rhs=vec[:, c0 : c0 + 512], start=True, stop=True)

        a3 = a_col[:].rearrange("p (u e) -> p u e", e=2).unsqueeze(1).to_broadcast([P, 256, 2, 2])
        n3 = a_neg[:].unsqueeze(1).to_broadcast([P, 256, 4])

        xt, hb, kb, sqt = {}, {}, {}, {}

        def x_turn(j):
            g, t0 = divmod(2 * j, 4)
            words = x_sb[g][:].bitcast(F32)
            ps = psum.tile([P, 2, 256], F32, tag="o", bufs=OB, name="xt")
            for b in range(2):
                for u in range(2):
                    nc.tensor.transpose(ps[:, u, b * P : b * P + P], words[:, t0 + b, u : 256 : 2], ident[:])
            xt[j] = ps[:].bitcast(BF16).rearrange("p u (r e) -> p r u e", e=2)

        def x_square(j):
            sqt[j] = work.tile([P, 256, 4], F32, tag="sq", bufs=2, name="sq")
            nc.scalar.activation(out=sqt[j][:].rearrange("p r (u e) -> p r u e", e=2), in_=xt[j], func=ACT.Square)

        def x_h(j):
            hb[j] = work.tile([P, 256, 4], BF16, tag="hb", bufs=2, align_bytes=64, name="hb")
            nc.vector.tensor_tensor(out=hb[j][:].rearrange("p r (u e) -> p r u e", e=2), in0=xt[j], in1=a3, op=ALU.mult)

        def x_k(j):
            kb[j] = work.tile([P, 256, 4], BF16, tag="kb", bufs=2, align_bytes=64, name="kb")
            nc.vector.scalar_tensor_tensor(out=kb[j][:], in0=sqt[j][:], scalar=1.0, in1=n3, op0=ALU.subtract, op1=ALU.mult)

        def h_quant(j):
            cols = slice(j * 256, j * 256 + 256)
            nc.vector.quantize_mx(out=h_codes[:, cols].bitcast(FP8X4), scales=h_scales[:, cols], in_=hb[j][:].rearrange("p r t -> p (r t)"))

        def k_quant(j):
            cols = slice(j * 256, j * 256 + 256)
            nc.vector.quantize_mx(out=k_codes[:, cols].bitcast(FP8X4), scales=k_scales[:, cols], in_=kb[j][:].rearrange("p r t -> p (r t)"))

        il = {}

        def mp_inter(name, c, engine):
            t = work.tile([P, 512, 4], BF16, tag="ob" if engine == "V" else "il" + engine, bufs=2 if engine == "V" else ILB, align_bytes=64, name="il")
            interleave(engine, t[:], raw[(name, c)])
            il[(name, c)] = t

        def mp_quant(name, c):
            codes, scales = (m_codes, m_scales) if name == "m" else (p_codes, p_scales)
            cols = slice(c * 512, c * 512 + 512)
            nc.vector.quantize_mx(out=codes[:, cols].bitcast(FP8X4), scales=scales[:, cols], in_=il[(name, c)][:].rearrange("p c t -> p (c t)"))

        w_raw = {}

        def w_load(q):
            r = work.tile([P, 4, 1024], BF16, tag="raw", bufs=4, name="raw")
            nc.sync.dma_start(out=r[:], in_=w_view[q])
            for h in range(2):
                w_raw[(q, h)] = r[:, :, h * 512 : h * 512 + 512]

        def w_inter(q, h, engine):
            t = work.tile([P, 512, 4], BF16, tag="il" + engine, bufs=ILB, align_bytes=64, name="il")
            interleave(engine, t[:], w_raw[(q, h)])
            il[("w", q, h)] = t

        def w_quant(q, h):
            cols = slice(h * 512, h * 512 + 512)
            nc.vector.quantize_mx(out=w_codes[:, q, cols].bitcast(FP8X4), scales=w_scales[:, q, cols], in_=il[("w", q, h)][:].rearrange("p c t -> p (c t)"))

        qt, stat, rb, rt, rq, o32, ac = {}, {}, {}, {}, {}, {}, {}

        zt = {}

        def logits(b, c):
            z = psum.tile([P, CHUNK], F32, tag="z", bufs=ZB, name="z")
            rows = slice(b * P, b * P + P)
            cols = slice(c * CHUNK, c * CHUNK + CHUNK)
            nc.tensor.matmul_mx(out=z[:], lhsT=h_codes[:, rows].bitcast(FP8X4), lhsT_scale=h_scales[:, rows], rhs=m_codes[:, cols].bitcast(FP8X4), rhs_scale=m_scales[:, cols], start=True, stop=False)
            nc.tensor.matmul_mx(out=z[:], lhsT=k_codes[:, rows].bitcast(FP8X4), lhsT_scale=k_scales[:, rows], rhs=p_codes[:, cols].bitcast(FP8X4), rhs_scale=p_scales[:, cols], start=False, stop=True)
            zt[(b, c)] = z

        def addlp(b, c):
            if b not in qt:
                qt[b] = work.tile([P, C], F32, tag="q", bufs=6, name="q")
            cols = slice(c * CHUNK, c * CHUNK + CHUNK)
            nc.vector.tensor_tensor(out=qt[b][:, cols], in0=zt[(b, c)][:], in1=lp_all[:, cols], op=ALU.add)

        def rowmax(b):
            nm = work.tile([P, 1], F32, tag="nm", bufs=4, name="nm")
            nc.vector.tensor_reduce(out=nm[:], in_=qt[b][:], axis=AX.X, op=ALU.max, negate=True)
            stat[b] = nm

        def expo(b):
            s = work.tile([P, 1], F32, tag="ssum", bufs=4, name="ssum")
            nc.scalar.activation(out=qt[b][:], in_=qt[b][:], func=ACT.Exp, bias=stat[b][:], scale=1.0, accum_out=s[:])
            stat[b] = s

        def recip(b):
            r = work.tile([P, 1], F32, tag="rs", bufs=4, name="rs")
            nc.vector.reciprocal(out=r[:], in_=stat[b][:])
            stat[b] = r

        def norm(b, h, engine):
            cols = slice(0, C)
            if engine == "S":
                nc.scalar.activation(out=qt[b][:, cols], in_=qt[b][:, cols], func=ACT.Identity, bias=minus[:], scale=stat[b][:])
            else:
                for c0 in range(0, C, NSTEP):
                    cols = slice(c0, c0 + NSTEP)
                    nc.gpsimd.tensor_scalar(out=qt[b][:, cols], in0=qt[b][:, cols], scalar1=stat[b][:], scalar2=-1.0 / C, op0=ALU.mult, op1=ALU.add)

        def gain(b, h):
            if b not in rb:
                rb[b] = work.tile([P, C], BF16, tag="rb", bufs=2, name="rb")
            lo = h * 1024
            mid = lo + 1024 - GG.get((b, h), 0)
            nc.vector.tensor_tensor(out=rb[b][:, lo:mid], in0=qt[b][:, lo:mid], in1=gc_ps[h][:, 0 : mid - lo], op=ALU.mult)

        def gain_g(b, h):
            if b not in rb:
                rb[b] = work.tile([P, C], BF16, tag="rb", bufs=2, name="rb")
            hi = h * 1024 + 1024
            mid = hi - GG[(b, h)]
            nc.gpsimd.tensor_tensor(out=rb[b][:, mid:hi], in0=qt[b][:, mid:hi], in1=gc_all[:, mid:hi], op=ALU.mult)

        tp = {}

        def turn(b, h):
            if b not in rt:
                rt[b] = work.tile([P, PASSES, P, 4], BF16, tag="rt", bufs=2, align_bytes=64, name="rt")
            words = rb[b][:].bitcast(F32)
            ps = psum.tile([P, 2, 2, P], F32, tag="tr", bufs=TB, name="rtp")
            for s in range(2):
                for u in range(2):
                    w0 = 256 * (2 * h + s)
                    nc.tensor.transpose(ps[:, s, u, :], words[:, w0 + u : w0 + 256 : 2], ident[:])
            tp[(b, h)] = ps

        def turned(b, h):
            ps = tp[(b, h)]
            nc.scalar.copy(out=rt[b][:, 2 * h : 2 * h + 2].bitcast(F32), in_=ps[:].rearrange("p s u r -> p s r u"))

        def rquant(b, h):
            if b not in rq:
                rq[b] = (work.tile([P, 512], U32, tag="rc", bufs=4, align_bytes=64, name="rc"), work.tile([P, 512], U8, tag="rsc", bufs=4, align_bytes=64, name="rsc"))
            codes, scales = rq[b]
            cols = slice(h * 256, h * 256 + 256)
            nc.vector.quantize_mx(out=codes[:, cols].bitcast(FP8X4), scales=scales[:, cols], in_=rt[b][:, 2 * h : 2 * h + 2].rearrange("p q r t -> p (q r t)"))

        def second(b, h):
            g, t = divmod(b, 4)
            codes, scales = rq[b]
            acc = psum.tile([P, 512], F32, tag="o", bufs=OB, name="acc")
            ac[(b, h)] = acc
            oc = slice(h * 512, h * 512 + 512)
            for q in range(PASSES):
                cols = slice(q * P, q * P + P)
                nc.tensor.matmul_mx(out=acc[:], lhsT=codes[:, cols].bitcast(FP8X4), lhsT_scale=scales[:, cols], rhs=w_codes[:, q, oc].bitcast(FP8X4), rhs_scale=w_scales[:, q, oc], start=(q == 0), stop=(q == PASSES - 1))

        def drain(b, h, engine="S"):
            g, t = divmod(b, 4)
            if (g, h) not in o32:
                o32[(g, h)] = work.tile([P, 4, 512], F32, tag="raw", bufs=4, name="o32")
            if engine == "S":
                nc.scalar.copy(out=o32[(g, h)][:, t, :], in_=ac[(b, h)][:])
            else:
                nc.vector.tensor_copy(out=o32[(g, h)][:, t, :], in_=ac[(b, h)][:])
            rows = out_0[g * 512 : g * 512 + 512, :].rearrange("(p t) o -> p t o", t=4)
            nc.sync.dma_start(out=rows[:, t, h * 512 : h * 512 + 512], in_=o32[(g, h)][:, t, :])

        obt = {}

        def o_inter(g, h, engine, lo=0, hi=512):
            if (g, h) not in obt:
                ob = work.tile([P, 512, 4], BF16, tag="ob", bufs=2, align_bytes=64, name="ob")
                obt[(g, h)] = ob
            interleave(engine, obt[(g, h)][:, lo:hi, :], o32[(g, h)][:, :, lo:hi])

        def o_quant(g, h):
            ob = obt[(g, h)]
            oc = work.tile([P, 512], U32, tag="oc", bufs=2, align_bytes=64, name="oc")
            osc = work.tile([P, 512], U8, tag="os", bufs=2, align_bytes=64, name="os")
            nc.vector.quantize_mx(out=oc[:].bitcast(FP8X4), scales=osc[:], in_=ob[:].rearrange("p c t -> p (c t)"))
            cols = slice(h * 512, h * 512 + 512)
            nc.sync.dma_start(out=out_1[g][:, cols, :].rearrange("p m t -> p (m t)").bitcast(I32), in_=oc[:].bitcast(I32))
            for quad in range(4):
                nc.sync.dma_start(out=out_2[g, 4 * quad : 4 * quad + 4, cols].bitcast(I32), in_=osc[32 * quad : 32 * quad + 4, :].bitcast(I32))


        x1 = work.tile([P, 4, D], BF16, tag="x", bufs=2)
        x_sb.append(x1)
        load_q, tensor_q, scalar_q, gpsimd_q, vector_q = [], [], [], [], []

        def put(queue, name, call, *needs):
            queue.append((name, needs, call))

        def T(name, call, *needs):
            put(tensor_q, name, call, *needs)

        def S(name, call, *needs):
            put(scalar_q, name, call, *needs)

        def G(name, call, *needs):
            put(gpsimd_q, name, call, *needs)

        def V(name, call, *needs):
            put(vector_q, name, call, *needs)

        put(load_q, "x1", lambda: nc.sync.dma_start(out=x1[:], in_=x_view[1]), ("xt", 0), ("xt", 1))
        for q in range(PASSES):
            put(load_q, ("wl", q), lambda q=q: w_load(q), ("I", "m", q), ("I", "p", q))

        def t_xt(j):
            T(("xt", j), lambda: x_turn(j), *(["x1"] if j >= 2 else []), *([("sq", j - 2), ("h", j - 2)] if j >= 2 else []))

        def t_z(b, c):
            T(("z", b, c), lambda: logits(b, c), ("qh", b // 2), ("qk", b // 2), ("Q", "m", c), ("Q", "p", c))

        def t_turn(b, h):
            T(("t", b, h), lambda: turn(b, h), *([("d", b, h)] if GG.get((b, h), 0) < 1024 else []), *([("dg", b, h)] if (b, h) in GG else []))

        def t_second(b, h):
            T(("o", b, h), lambda: second(b, h), ("qr", b, 0), ("qr", b, 1), *[("Qw", q, h) for q in range(PASSES)])

        def s_sq(j):
            S(("sq", j), lambda: x_square(j), ("xt", j))

        def inter_mp(fn, engine, name, c):
            fn(("I", name, c), lambda: mp_inter(name, c, engine))

        def inter_w(fn, engine, q, h):
            fn(("iw", q, h), lambda: w_inter(q, h, engine), ("wl", q))

        def s_exp(b):
            S(("e", b), lambda: expo(b), ("m", b))

        def s_turned(b, h):
            S(("tc", b, h), lambda: turned(b, h), ("t", b, h))

        def s_drain(b, h):
            S(("dr", b, h), lambda: drain(b, h), ("o", b, h))

        def inter_o(fn, engine, g, h, lo=0, hi=512):
            fn(("io", g, h, lo), lambda: o_inter(g, h, engine, lo, hi), *[("dr", 4 * g + t, h) for t in range(4)])

        def norms(fn, engine, b, h):
            fn(("n", b, h), lambda: norm(b, h, engine), ("r", b))

        def g_gain(b, h):
            G(("dg", b, h), lambda: gain_g(b, h), ("n", b, 0), "gccopy")

        def v_h(j):
            V(("h", j), lambda: x_h(j), ("xt", j))

        def v_k(j):
            V(("k", j), lambda: x_k(j), ("sq", j))

        def v_qh(j):
            V(("qh", j), lambda: h_quant(j), ("h", j))

        def v_qk(j):
            V(("qk", j), lambda: k_quant(j), ("k", j))

        def v_q(name, c):
            V(("Q", name, c), lambda: mp_quant(name, c), ("I", name, c))

        def v_a(b, c):
            V(("a", b, c), lambda: addlp(b, c), ("z", b, c), "lp0" if c < 2 else "lp1")

        def v_max(b):
            V(("m", b), lambda: rowmax(b), *[("a", b, c) for c in range(CHUNKS)])

        def v_recip(b):
            V(("r", b), lambda: recip(b), ("e", b))

        def v_gain(b, h):
            V(("d", b, h), lambda: gain(b, h), ("n", b, 0), "gcps")

        def v_qr(b, h):
            V(("qr", b, h), lambda: rquant(b, h), ("tc", b, h))

        def v_qw(q, h):
            V(("Qw", q, h), lambda: w_quant(q, h), ("iw", q, h))

        def v_qo(g, h, *los):
            V(("qo", g, h), lambda: o_quant(g, h), *[("io", g, h, lo) for lo in los])

        LAG = 4
        t_xt(0)
        t_xt(1)
        T("lpps", spread_lp)
        for c in range(CHUNKS):
            for b in range(4):
                t_z(b, c)
            if c == 1:
                t_xt(2)
            if c == 2:
                T("gcps", spread_gc)
                t_xt(3)
        for i in range(BLOCKS + 2):
            n = i + LAG
            if n < BLOCKS:
                t_z(n, 0)
                t_z(n, 1)
                t_z(n, 2)
            if i >= 2:
                t_second(i - 2, 0)
            if i < BLOCKS:
                t_turn(i, 0)
            if n < BLOCKS:
                t_z(n, 3)
            if i >= 2:
                t_second(i - 2, 1)
            if i < BLOCKS:
                t_turn(i, 1)

        s_sq(0)
        s_sq(1)
        inter_mp(S, "S", "m", 0)
        S("lp0", lambda: lp_copy(0), "lpps")
        S("lp1", lambda: lp_copy(1), "lpps")
        inter_mp(S, "S", "m", 1)
        inter_mp(S, "S", "p", 1)
        inter_mp(S, "S", "p", 2)
        inter_mp(S, "S", "m", 2)
        s_sq(2)
        inter_mp(S, "S", "m", 3)
        inter_w(S, "S", 0, 0)
        s_sq(3)
        inter_w(S, "S", 0, 1)
        inter_w(S, "S", 1, 0)
        s_exp(0)
        S("gccopy", lambda: (gc_copy(0), gc_copy(1)), "gcps")
        inter_w(S, "S", 1, 1)
        s_exp(1)
        inter_w(S, "S", 2, 0)
        s_exp(2)
        s_exp(3)
        for i in range(BLOCKS + 2):
            if i < BLOCKS:
                s_turned(i, 0)
            if i >= 2:
                s_drain(i - 2, 0)
                if i < BLOCKS + 1:
                    s_drain(i - 2, 1)
            if i < BLOCKS:
                s_turned(i, 1)
            if i == 0:
                inter_w(S, "S", 2, 1)
            if i + LAG < BLOCKS:
                s_exp(i + LAG)
        inter_o(S, "S", 1, 0, 320, 512)
        inter_o(S, "S", 1, 1, 320, 512)

        inter_mp(G, "G", "p", 3)
        for b in range(BLOCKS):
            norms(G, "G", b, 0)
            if (b, 1) in GG:
                g_gain(b, 1)
            if b < 2:
                inter_w(G, "G", 3, b)
        inter_o(G, "G", 0, 1)

        v_h(0)
        v_h(1)
        v_qh(0)
        v_qh(1)
        V(("I", "p", 0), lambda: mp_inter("p", 0, "V"))
        v_k(0)
        v_k(1)
        v_qk(0)
        v_qk(1)
        v_q("p", 0)
        v_q("m", 0)
        for b in range(4):
            v_a(b, 0)
        v_q("m", 1)
        v_q("p", 1)
        for b in range(4):
            v_a(b, 1)
        v_h(2)
        v_q("p", 2)
        v_q("m", 2)
        v_k(2)
        for b in range(4):
            v_a(b, 2)
        v_qh(2)
        v_q("m", 3)
        v_q("p", 3)
        v_a(0, 3)
        v_a(1, 3)
        v_h(3)
        v_max(0)
        v_a(2, 3)
        v_a(3, 3)
        v_qk(2)
        v_k(3)
        v_qh(3)
        v_max(1)
        v_qw(0, 0)
        v_qw(0, 1)
        v_recip(0)
        v_max(2)
        v_qk(3)
        v_qw(1, 0)
        v_recip(1)
        v_max(3)
        late_w = {0: ((1, 1), (2, 0)), 1: ((3, 0), (2, 1), (3, 1))}
        for i in range(BLOCKS):
            n = i + LAG
            v_gain(i, 0)
            if n < BLOCKS:
                v_a(n, 0)
                v_a(n, 1)
            if i < 6:
                v_recip(i + 2)
            v_gain(i, 1)
            if n < BLOCKS:
                v_a(n, 2)
                v_a(n, 3)
            if i >= 1:
                v_qr(i - 1, 0)
                v_qr(i - 1, 1)
            for q, h in late_w.get(i, ()):
                v_qw(q, h)
            if n < BLOCKS:
                v_max(n)
        v_qr(7, 0)
        v_qr(7, 1)
        inter_o(V, "V", 0, 0)
        v_qo(0, 0, 0)
        v_qo(0, 1, 0)
        inter_o(V, "V", 1, 0, 0, 320)
        V(("dr", 7, 1), lambda: drain(7, 1, "V"), ("o", 7, 1))
        inter_o(V, "V", 1, 1, 0, 320)
        v_qo(1, 0, 0, 320)
        v_qo(1, 1, 0, 320)


        def ring(seq, n, freed_by):
            for later, earlier in zip(seq[n:], seq):
                extra.setdefault(later, []).extend(freed_by(earlier))

        extra = {}
        t_order = [task[0] for task in tensor_q]
        s_order = [task[0] for task in scalar_q]
        g_order = [task[0] for task in gpsimd_q]
        v_order = [task[0] for task in vector_q]
        ring([k for k in t_order if k[0] == "z"], ZB, lambda k: [("a",) + k[1:]])
        extra.setdefault([k for k in t_order if k[0] == "z"][ZB - 2], []).extend(["lp0", "lp1"])
        ring([k for k in t_order if k[0] == "t"], TB, lambda k: [("tc",) + k[1:]])
        ring([k for k in t_order if k[0] == "o"], OB, lambda k: [("dr",) + k[1:]])
        for k in [k for k in t_order if k[0] == "o"][:2]:
            extra.setdefault(k, []).extend([("sq", 2), ("sq", 3), ("h", 2), ("h", 3)])
        for order in (s_order, g_order):
            ring([k for k in order if k[0] in ("I", "iw")], ILB, lambda k: [("Q",) + k[1:]] if k[0] == "I" else [("Qw",) + k[1:]])
        ring([k for k in s_order if k[0] == "sq"], 2, lambda k: [("k", k[1])])
        ring([k for k in v_order if k[0] == "h"], 2, lambda k: [("qh", k[1])])
        ring([k for k in v_order if k[0] == "k"], 2, lambda k: [("qk", k[1])])
        for b in range(2, BLOCKS):
            for h in range(2):
                extra.setdefault(("d", b, h), []).extend([("t", b - 2, 0), ("t", b - 2, 1)])
                extra.setdefault(("dg", b, h), []).extend([("t", b - 2, 0), ("t", b - 2, 1)])
                extra.setdefault(("t", b, h), []).extend([("qr", b - 2, 0), ("qr", b - 2, 1)])
                if b >= 4:
                    extra.setdefault(("qr", b, h), []).extend([("o", b - 4, 0), ("o", b - 4, 1)])
            if b >= 4:
                extra.setdefault(("m", b), []).append(("e", b - 4))
                extra.setdefault(("e", b), []).append(("r", b - 4))
                extra.setdefault(("r", b), []).append(("n", b - 4, 0))
            if b >= QB:
                for c in range(CHUNKS):
                    extra.setdefault(("a", b, c), []).extend([k for k in v_order + g_order if k[0] in ("d", "dg") and k[1] == b - QB])
        for h in range(2):
            for lo in (0, 320):
                extra[("io", 1, h, lo)] = [("qo", 0, h)]
        done = set()
        queues = [load_q, tensor_q, scalar_q, gpsimd_q, vector_q]
        while any(queues):
            before = len(done)
            for queue in queues:
                while queue and all(need in done for need in (*queue[0][1], *extra.get(queue[0][0], []))):
                    name, needs, call = queue.pop(0)
                    call()
                    done.add(name)
            assert len(done) > before, [q[0][:2] for q in queues if q]
